import numpy as np
import ml_dtypes


def mxq(x, axis, fmt="e4m3"):
    dtype, down = {"e4m3": (ml_dtypes.float8_e4m3fn, 7), "e5m2": (ml_dtypes.float8_e5m2, 14)}[fmt]
    v = np.moveaxis(np.asarray(x, np.float32).astype(ml_dtypes.bfloat16).astype(np.float64), axis, -1)
    blocks = v.reshape(v.shape[:-1] + (-1, 32))
    amax = np.abs(blocks).max(-1, keepdims=True)
    byte = np.maximum(np.where(amax > 0, np.frexp(amax)[1] - 1 + 127, 0) - down, 1)
    scale = np.exp2(byte - 127.0)
    codes = (blocks / scale).astype(np.float32).astype(dtype).astype(np.float64)
    return np.moveaxis((codes * scale).reshape(v.shape), -1, axis)


WIDE = False


def mx_kscale(k):
    if not WIDE:
        return np.ones(k)
    levels = np.array([10, -10, 5, -5, 0])
    if k % 512:
        return np.exp2(np.random.permutation(np.resize(levels, k // 32))).repeat(32)
    a = np.empty((k // 512, 16))
    for p in range(k // 512):
        a[p, :8] = np.random.permutation(np.resize(levels, 8))
        for g in range(8):
            far = levels[np.abs(levels - a[p, g]) >= 10]
            a[p, g + 8] = far[np.random.randint(len(far))]
    return np.exp2(a.ravel()).repeat(32)


def f64(x):
    return np.asarray(x).astype(np.float64)


def striped(idx):
    return np.tile(idx.reshape(-1, 16).T, (8, 1)).astype(np.uint16)


def unstriped(offs):
    return offs[:16].T.reshape(-1).astype(np.int64)


E2M1 = np.array([0.0, 0.5, 1.0, 1.5, 2.0, 3.0, 4.0, 6.0, -0.0, -0.5, -1.0, -1.5, -2.0, -3.0, -4.0, -6.0])


def pack_weight(w, fmt):
    k, n = w.shape
    w = f64(np.asarray(w, np.float32).astype(ml_dtypes.bfloat16)).reshape(k // 32, 32, n)
    amax = np.abs(w).max(1)
    if fmt == "e4m3":
        byte = np.frexp(amax)[1] - 1 + 127 - 7
    else:
        mant, ex = np.frexp(amax / 6.0)
        byte = np.where(mant > 0.5, ex, ex - 1) + 127
    byte = np.clip(np.where(amax > 0, byte, 1), 1, 254)
    scaled = (w * np.exp2(127.0 - byte)[:, None, :]).reshape(k, n).astype(np.float32)
    by_word = np.ascontiguousarray(scaled.reshape(k // 512, 128, 4, n).transpose(0, 1, 3, 2))
    if fmt == "e4m3":
        words = by_word.astype(ml_dtypes.float8_e4m3fn).view(np.uint8)
    else:
        c = by_word.astype(ml_dtypes.float4_e2m1fn).view(np.uint8) & 0xF
        words = (c[..., 0::2] | (c[..., 1::2] << 4)).reshape(k // 512, 128, 2 * n)
    return np.ascontiguousarray(words), np.ascontiguousarray(byte.astype(np.uint8).reshape(k // 512, 16, n))


def unpack_weight(words, scales, fmt):
    g, _, n = scales.shape
    words = np.ascontiguousarray(words).reshape(g, 128, n, -1)
    if fmt == "e4m3":
        vals = words.view(ml_dtypes.float8_e4m3fn).astype(np.float64)
    else:
        nib = np.empty((g, 128, n, 4), np.uint8)
        nib[..., 0::2] = words & 0xF
        nib[..., 1::2] = words >> 4
        vals = E2M1[nib]
    vals = vals * np.repeat(np.exp2(scales.astype(np.float64) - 127.0), 8, axis=1)[..., None]
    return vals.transpose(0, 1, 3, 2).reshape(g * 512, n)


def gelu(v):
    return 0.5 * v * (1.0 + np.tanh(np.sqrt(2.0 / np.pi) * (v + 0.044715 * v**3)))


K, H, T, S, T2, P = 1024, 1024, 2048, 512, 1024, 512


def setup_inputs():
    n = np.random.standard_normal
    s = mx_kscale(K)[:, None]
    u = mx_kscale(H)[:, None]
    d = {}
    d["tab_words"], d["tab_scales"] = pack_weight(n((K, T)) * s, "e4m3")
    d["offs"] = striped(np.random.permutation(T)[:S])
    d["w1"] = (n((K, H)) / s * u.T / K**0.5).astype(np.float32)
    d["w2_words"], d["w2_scales"] = pack_weight(n((K, H)) / s * u.T / K**0.5, "e2m1")
    d["w3_words"], d["w3_scales"] = pack_weight(n((K, H)) / s * u.T / K**0.5, "e4m3")
    d["wgs"] = np.exp(0.3 * n((128, S))).astype(np.float32)
    d["page0"] = (n((H, T2)) * u).astype(np.float32)
    d["offs2"] = striped(np.random.permutation(T2)[:S])
    d["offs3"] = striped(np.random.permutation(T2)[:P])
    d["gv"] = (n(H) / u[:, 0]**2 / H**0.5).astype(np.float32)
    d["ref"] = n((T2, P)).astype(np.float32)
    return d


def reference(tab_words, tab_scales, offs, w1, w2_words, w2_scales, w3_words, w3_scales,
              wgs, page0, offs2, offs3, gv, ref):
    v = unpack_weight(tab_words, tab_scales, "e4m3")[:, unstriped(offs)]
    f1 = mxq(f64(w1), 0, "e4m3").T @ v
    f2 = unpack_weight(w2_words, w2_scales, "e2m1").T @ v
    f3 = unpack_weight(w3_words, w3_scales, "e4m3").T @ v
    h = np.maximum(f1, np.minimum(f2, f3))
    page = f64(page0).copy()
    page[:, unstriped(offs2)] = np.tile(f64(wgs), (H // 128, 1)) * h
    x = np.abs(page[:, unstriped(offs3)]) * f64(gv)[:, None]
    e = mxq(page, 0, "e4m3").T @ mxq(x, 0, "e4m3")
    return np.exp(-np.abs(e - f64(ref)))

@@ -1,0 +1,311 @@
+from contextlib import ExitStack
+
+import concourse.mybir as mybir
+
+K, H, T, S, T2, NP = 1024, 1024, 2048, 512, 1024, 512
+FLOPS = 2 * (3 * K * H * S + H * T2 * NP)
+
+F32 = mybir.dt.float32
+BF16 = mybir.dt.bfloat16
+I32 = mybir.dt.int32
+U32 = mybir.dt.uint32
+U16 = mybir.dt.uint16
+U8 = mybir.dt.uint8
+FP8X4 = mybir.dt.float8_e4m3fn_x4
+FP4X4 = mybir.dt.float4_e2m1fn_x4
+ALU = mybir.AluOpType
+ACT = mybir.ActivationFunctionType
+
+P = 128
+PACK = 4
+PASS = P * PACK
+KP = K // PASS
+RP = H // PASS
+RUN = 4
+RUNS = P // RUN
+SLICES = RP * PACK
+BANKS = 8
+QUART = T2 // 4
+HB, LB, CB, VABS, DB, F1B, PB = 1, 2, 1, (1, 3, 5, 7), 4, 1, 2
+
+
+def tile_list_braille_cell_proofing_kernel(
+    tc, tab_words, tab_scales, offs, w1, w2_words, w2_scales, w3_words, w3_scales,
+    wgs, page0, offs2, offs3, gv, ref, out,
+):
+    nc = tc.nc
+    with ExitStack() as ctx:
+        keep = ctx.enter_context(tc.tile_pool(name="keep", bufs=1))
+        ring = ctx.enter_context(tc.tile_pool(name="ring", bufs=2))
+        psum = ctx.enter_context(tc.psum_pool(name="psum", bufs=1))
+
+        def bank_tile(n):
+            return psum.tile([P, 512], F32, name="bank%d" % n)
+
+        idx = keep.tile([P, S // 16], U16, name="idx")
+        idx2 = keep.tile([P, S // 16], U16, name="idx2")
+        idx3 = keep.tile([P, NP // 16], U16, name="idx3")
+
+        warm = keep.tile([P, 8], F32, name="warm")
+        warm_out = keep.tile([P, 8], F32, name="warm_out")
+
+        tab_s = keep.tile([P, KP * T], U8, name="tab_s", align_bytes=64)
+        w_s = keep.tile([P, KP * H], U8, name="w_s", align_bytes=64)
+        nc.vector.memset(tab_s[:].bitcast(I32), 0)
+        nc.vector.memset(w_s[:].bitcast(I32), 0)
+        v_s = [keep.tile([P, S], U8, name="v_s%d" % a, align_bytes=64) for a in range(KP)]
+        nc.vector.memset(warm[:], 0.0)
+        nc.scalar.activation(warm_out[:], warm[:], ACT.Exp)
+
+        def load_tab_words(a):
+            tile = keep.tile([P, T], I32, name="tab_w%d" % a, align_bytes=64)
+            nc.sync.dma_start(tile[:], tab_words[a].rearrange("p t i -> p (t i)").bitcast(I32))
+            return tile
+
+        def load_scale_rows(queue, tile, first_row, scales):
+            rows = scales.bitcast(I32).rearrange("a q c -> q a c")
+            for quad in range(4):
+                lo = 32 * quad + first_row
+                queue.dma_start(
+                    tile[lo : lo + 4, :].bitcast(I32).rearrange("p (a c) -> p a c", a=KP),
+                    rows[4 * quad : 4 * quad + 4],
+                )
+
+        def load_w2(b):
+            raw = keep.tile([P, KP, PASS // 2], I32, name="w2_raw%d" % b)
+            src = w2_words.bitcast(I32).rearrange("a p c -> p a c")
+            nc.sync.dma_start(raw[:], src[:, :, b * PASS // 2 : (b + 1) * PASS // 2])
+            return raw
+
+        def load_w3(b):
+            raw = keep.tile([P, KP, PASS], I32, name="w3_raw%d" % b)
+            src = w3_words.rearrange("a p c i -> a p (c i)").bitcast(I32).rearrange("a p c -> p a c")
+            nc.sync.dma_start(raw[:], src[:, :, b * PASS : (b + 1) * PASS])
+            return raw
+
+        def load_w1(a, b):
+            tile = ring.tile([P, PACK, PASS], F32, name="w1_raw", tag="w1_raw", bufs=4)
+            rows = w1[a * PASS : (a + 1) * PASS, b * PASS : (b + 1) * PASS]
+            nc.sync.dma_start(tile[:], rows.rearrange("(p j) c -> p j c", j=PACK))
+            return tile
+
+        def load_wgs(t):
+            tile = keep.tile([P, S], F32, name="wg%d" % t)
+            rows = wgs.rearrange("(u t i) j -> t u i j", t=PACK, i=RUN)[t]
+            for quad in range(4):
+                nc.sync.dma_start(tile[32 * quad : 32 * quad + 32, :], rows)
+            return tile
+
+        def load_page(s):
+            b, t = divmod(s, PACK)
+            tile = keep.tile([P, T2], F32, name="page%d" % s)
+            nc.sync.dma_start(tile[:], page0.rearrange("(b u t i) m -> b t u i m", b=RP, t=PACK, i=RUN)[b, t])
+            return tile
+
+        gv_run = keep.tile([P, RP, 16], F32, name="gv_run")
+
+        def load_gv():
+            rows = gv.rearrange("(b u c) -> u b c", b=RP, c=16)
+            for i in range(RUN):
+                nc.sync.dma_start(gv_run[i:P:RUN, :, 0:13], rows[:, :, i : i + 13])
+
+        def load_ref(half):
+            tile = ring.tile([P, PACK, PASS], F32, name="w1_raw", tag="w1_raw", bufs=4)
+            rows = ref[half * 512 : (half + 1) * 512, :].rearrange("(m p) j -> p m j", p=P)
+            nc.sync.dma_start(tile[:], rows)
+            return tile
+
+        nc.sync.dma_start(idx[:], offs)
+        load_scale_rows(nc.sync, tab_s, 0, tab_scales)
+        tab_w = [load_tab_words(0)]
+        tab_w.append(load_tab_words(1))
+        w3_raw = [load_w3(0)]
+        load_scale_rows(nc.sync, w_s, 4, w3_scales)
+        w2_raw = [load_w2(0)]
+        load_scale_rows(nc.sync, w_s, 0, w2_scales)
+        w1_raw = {(0, 0): load_w1(0, 0), (1, 0): load_w1(1, 0)}
+        nc.sync.dma_start(idx2[:], offs2)
+        wg = [load_wgs(0)]
+        page = [load_page(0)]
+        nc.sync.dma_start(idx3[:], offs3)
+        load_gv()
+        w3_raw.append(load_w3(1))
+        w2_raw.append(load_w2(1))
+        w1_raw[(0, 1)] = load_w1(0, 1)
+        w1_raw[(1, 1)] = load_w1(1, 1)
+        for t in range(1, PACK):
+            wg.append(load_wgs(t))
+            page.append(load_page(t))
+        for s in range(PACK, SLICES):
+            page.append(load_page(s))
+
+        for a in range(KP):
+            nc.vector.tensor_copy(v_s[a][:], tab_s[:, a * T : (a + 1) * T].indirect(idx[:]))
+        v_w = []
+        for a in range(KP):
+            words = keep.tile([P, S], I32, name="v_w%d" % a, align_bytes=64)
+            nc.vector.tensor_copy(words[:].bitcast(U32), tab_w[a][:].bitcast(U32).indirect(idx[:]))
+            v_w.append(words)
+
+        w_sd = keep.tile([P, RP * PACK * KP * P], U8, name="w_sd", align_bytes=64)
+        nc.vector.tensor_copy(
+            w_sd[:].bitcast(I32).rearrange("p (b t a u) -> p b t a u", b=RP, t=PACK, a=KP),
+            w_s[:].bitcast(I32).rearrange("p (a b u t) -> p b t a u", a=KP, b=RP, t=PACK),
+        )
+
+        def deal_w23(b):
+            raw2, raw3 = w2_raw[b], w3_raw[b]
+            d2 = keep.tile([P, PACK * KP * P // 2], I32, name="w2_d%d" % b, align_bytes=64)
+            d3 = keep.tile([P, PACK * KP * P], I32, name="w3_d%d" % b, align_bytes=64)
+            nc.vector.tensor_copy(
+                d2[:].rearrange("p (t a u i) -> p t a u i", t=PACK, a=KP, i=RUN // 2),
+                raw2[:].rearrange("p a (u t i) -> p t a u i", t=PACK, i=RUN // 2),
+            )
+            nc.vector.tensor_copy(
+                d3[:].rearrange("p (t a u i) -> p t a u i", t=PACK, a=KP, i=RUN),
+                raw3[:].rearrange("p a (u t i) -> p t a u i", t=PACK, i=RUN),
+            )
+            return d2, d3
+
+        staging = {}
+        for kind, s in [("w1", 0), ("f3", 0)] + [(kind, s) for s in range(1, SLICES) for kind in ("f3", "w1")]:
+            shape, dtype = ([P, KP, P * PACK], BF16) if kind == "w1" else ([P, S], F32)
+            staging[(kind, s)] = ring.tile(shape, dtype, name="staging", tag="staging", bufs=2, align_bytes=64)
+
+        def cast_w1(s):
+            b, t = divmod(s, PACK)
+            grouped = staging[("w1", s)]
+            for a in range(KP):
+                nc.scalar.copy(
+                    grouped[:, a, :].rearrange("p (u i j) -> p u i j", i=RUN, j=PACK),
+                    w1_raw[(a, b)][:].rearrange("p j (u t i) -> p t u i j", t=PACK, i=RUN)[:, t],
+                )
+            return grouped
+
+        def quantize(grouped_ap, width, name, bufs):
+            codes = ring.tile([P, width], U32, name=name + "_c", tag=name + "_c", bufs=bufs, align_bytes=64)
+            scales = ring.tile([P, width], U8, name=name + "_s", tag=name + "_s", bufs=bufs, align_bytes=64)
+            nc.vector.quantize_mx(out=codes[:].bitcast(FP8X4), scales=scales[:], in_=grouped_ap)
+            return codes, scales
+
+        def stage1_product(n, lhs_of_pass):
+            bank = bank_tile(n)
+            for a in range(KP):
+                codes, scales = lhs_of_pass(a)
+                nc.tensor.matmul_mx(
+                    out=bank[:], lhsT=codes, lhsT_scale=scales,
+                    rhs=v_w[a][:].bitcast(FP8X4), rhs_scale=v_s[a][:],
+                    start=(a == 0), stop=(a == KP - 1),
+                )
+            return bank
+
+        def lower_of_f2_f3(s):
+            b, t = divmod(s, PACK)
+            d2, d3 = w23_d[b]
+
+            def w2_of(a):
+                n = t * KP + a
+                m = s * KP + a
+                return (d2[:].bitcast(U8)[:, n * 2 * P : (n + 1) * 2 * P].bitcast(FP4X4), w_sd[:, m * P : (m + 1) * P])
+
+            def w3_of(a):
+                n = t * KP + a
+                m = s * KP + a
+                return (d3[:, n * P : (n + 1) * P].bitcast(FP8X4), w_sd[4:P, m * P : (m + 1) * P])
+
+            f3 = stage1_product(2 * (s % 2), w3_of)
+            f2 = stage1_product(2 * (s % 2) + 1, w2_of)
+            f3_sb = staging[("f3", s)]
+            nc.scalar.copy(f3_sb[:], f3[:])
+            low = ring.tile([P, S], F32, name="low", tag="low", bufs=LB)
+            nc.vector.tensor_tensor(low[:], f2[:], f3_sb[:], ALU.min)
+            return low
+
+        def quantize_w1(grouped):
+            return quantize(grouped[:].rearrange("p a c -> p (a c)"), KP * P, "w1", CB)
+
+        def features(s, quantized, low):
+            codes, scales = quantized
+            f1 = stage1_product(
+                4 + s % F1B,
+                lambda a: (codes[:, a * P : (a + 1) * P].bitcast(FP8X4), scales[:, a * P : (a + 1) * P])
+            )
+            if s == SLICES - 1:
+                h = ring.tile([P, S], F32, name="h_last", tag="page_il3", bufs=1, align_bytes=64)
+            else:
+                h = ring.tile([P, S], F32, name="h", tag="h", bufs=HB)
+            nc.vector.tensor_tensor(h[:], f1[:], low[:], ALU.max)
+            return h
+
+        gv_cols = gv_run[:, :, 0:13:PACK]
+        gv_pos = keep.tile([P, RP, PACK], F32, name="gv_pos")
+        gv_sign = keep.tile([P, RP, PACK], F32, name="gv_sign")
+
+        def interleave(copy, planes, columns, name):
+            grouped = ring.tile([P, columns.stop - columns.start, PACK], BF16, name=name, tag=name, bufs=1, align_bytes=64)
+            copy(
+                grouped[:].rearrange("p (c i) t -> p c t i", i=4),
+                planes[:, :, columns].rearrange("p t (c i) -> p c t i", i=4),
+            )
+            return grouped[:].rearrange("p c t -> p (c t)")
+
+        w23_d = [deal_w23(0)]
+        lows = [lower_of_f2_f3(0)]
+        w1_q = [quantize_w1(cast_w1(0))]
+        hs = [features(0, w1_q[0], lows[0])]
+        for s in range(1, 3):
+            lows.append(lower_of_f2_f3(s))
+            w1_q.append(quantize_w1(cast_w1(s)))
+
+        page_q, x_q, page_bf, x_bf = [], [], [], []
+        for s in range(SLICES):
+            b, t = divmod(s, PACK)
+            if t == 0:
+                page_bf.append(keep.tile([P, PACK, T2], BF16, name="page_bf%d" % b))
+                x_bf.append(keep.tile([P, PACK, NP], BF16, name="x_bf%d" % b))
+            nc.vector.tensor_tensor(page[s][:].indirect(idx2[:]), hs[s][:], wg[t][:], ALU.mult)
+            if s + 1 < SLICES:
+                hs.append(features(s + 1, w1_q[s + 1], lows[s + 1]))
+            if s == 0:
+                w23_d.append(deal_w23(1))
+                nc.vector.tensor_scalar(gv_pos[:], gv_cols, 0.0, 2.0, ALU.is_ge, ALU.mult)
+                nc.vector.tensor_scalar(gv_sign[:], gv_pos[:], 1.0, -1.0, ALU.mult, ALU.add)
+            if s + 3 < SLICES:
+                lows.append(lower_of_f2_f3(s + 3))
+                w1_q.append(quantize_w1(cast_w1(s + 3)))
+            nc.scalar.activation(page_bf[b][:, t, :], page[s][:], ACT.Copy, scale=gv_sign[:, b, t : t + 1])
+            picked = ring.tile([P, NP], F32, name="picked", tag="picked", bufs=PB)
+            nc.vector.tensor_copy(picked[:], page[s][:].indirect(idx3[:]))
+            nc.scalar.activation(x_bf[b][:, t, :], picked[:], ACT.Abs, scale=gv_run[:, b, PACK * t : PACK * t + 1])
+            if s in (PACK, SLICES - 1):
+                b = len(x_q)
+                first = nc.scalar.copy if b == 0 else nc.vector.tensor_copy
+                parts = [interleave(first, page_bf[b], slice(0, QUART), "page_il0")]
+                x_il = interleave(first, x_bf[b], slice(0, NP), "x_il")
+                for n in range(1, 4):
+                    parts.append(interleave(nc.scalar.copy, page_bf[b], slice(n * QUART, (n + 1) * QUART), "page_il%d" % n))
+                x_q.append(quantize(x_il, NP, "x", 2))
+                page_q.append([quantize(part, QUART, "page", 8) for part in parts])
+
+        ref_sb = [load_ref(0), load_ref(1)]
+        scores = [bank_tile(m) for m in range(T2 // P)]
+        for b in range(RP):
+            for m in range(T2 // P):
+                codes, scales = page_q[b][m // 2]
+                cols = slice((m % 2) * P, (m % 2 + 1) * P)
+                nc.tensor.matmul_mx(
+                    out=scores[m][:], lhsT=codes[:, cols].bitcast(FP8X4), lhsT_scale=scales[:, cols],
+                    rhs=x_q[b][0][:].bitcast(FP8X4), rhs_scale=x_q[b][1][:],
+                    start=(b == 0), stop=(b == RP - 1),
+                )
+        for m in range(T2 // P):
+            diff = ring.tile([P, NP], F32, name="diff", tag="diff", bufs=DB)
+            nc.vector.tensor_tensor(diff[:], scores[m][:], ref_sb[m // 4][:, m % 4, :], ALU.subtract)
+            size = ring.tile([P, NP], F32, name="size", tag="size", bufs=DB)
+            if m not in VABS:
+                nc.scalar.activation(size[:], diff[:], ACT.Abs)
+            else:
+                nc.vector.scalar_tensor_tensor(size[:], diff[:], -1.0, diff[:], ALU.mult, ALU.max)
+            result = ring.tile([P, NP], F32, name="result", tag="result", bufs=DB)
+            nc.scalar.activation(result[:], size[:], ACT.Exp, scale=-1.0)
+            nc.sync.dma_start(out[m * P : (m + 1) * P, :], result[:])

@@ -26,7 +26,7 @@ RUNS = P // RUN
 SLICES = RP * PACK
 BANKS = 8
 QUART = T2 // 4
-HB, LB, CB, VABS, DB, F1B, PB = 1, 2, 1, (1, 3, 5, 7), 4, 1, 2
+HB, LB, CB, VABS, DB, F1B, PB, FB, WB = 1, 1, 1, (1, 3, 5, 7), 4, 1, 2, 1, 1
 
 
 def tile_list_braille_cell_proofing_kernel(
@@ -50,9 +50,11 @@ def tile_list_braille_cell_proofing_kernel(
         warm_out = keep.tile([P, 8], F32, name="warm_out")
 
         tab_s = keep.tile([P, KP * T], U8, name="tab_s", align_bytes=64)
-        w_s = keep.tile([P, KP * H], U8, name="w_s", align_bytes=64)
+        w2_s = keep.tile([P, KP * H], U8, name="w2_s", align_bytes=64)
+        w3_s = keep.tile([P, KP * H], U8, name="w3_s", align_bytes=64)
         nc.vector.memset(tab_s[:].bitcast(I32), 0)
-        nc.vector.memset(w_s[:].bitcast(I32), 0)
+        nc.vector.memset(w3_s[:].bitcast(I32), 0)
+        nc.vector.memset(w2_s[:].bitcast(I32), 0)
         v_s = [keep.tile([P, S], U8, name="v_s%d" % a, align_bytes=64) for a in range(KP)]
         nc.vector.memset(warm[:], 0.0)
         nc.scalar.activation(warm_out[:], warm[:], ACT.Exp)
@@ -89,11 +91,11 @@ def tile_list_braille_cell_proofing_kernel(
             nc.sync.dma_start(tile[:], rows.rearrange("(p j) c -> p j c", j=PACK))
             return tile
 
-        def load_wgs(t):
+        def load_wgs(queue, t):
             tile = keep.tile([P, S], F32, name="wg%d" % t)
             rows = wgs.rearrange("(u t i) j -> t u i j", t=PACK, i=RUN)[t]
             for quad in range(4):
-                nc.sync.dma_start(tile[32 * quad : 32 * quad + 32, :], rows)
+                queue.dma_start(tile[32 * quad : 32 * quad + 32, :], rows)
             return tile
 
         def load_page(s):
@@ -107,7 +109,7 @@ def tile_list_braille_cell_proofing_kernel(
         def load_gv():
             rows = gv.rearrange("(b u c) -> u b c", b=RP, c=16)
             for i in range(RUN):
-                nc.sync.dma_start(gv_run[i:P:RUN, :, 0:13], rows[:, :, i : i + 13])
+                nc.gpsimd.dma_start(gv_run[i:P:RUN, :, 0:13], rows[:, :, i : i + 13])
 
         def load_ref(half):
             tile = ring.tile([P, PACK, PASS], F32, name="w1_raw", tag="w1_raw", bufs=4)
@@ -120,21 +122,22 @@ def tile_list_braille_cell_proofing_kernel(
         tab_w = [load_tab_words(0)]
         tab_w.append(load_tab_words(1))
         w3_raw = [load_w3(0)]
-        load_scale_rows(nc.sync, w_s, 4, w3_scales)
+        load_scale_rows(nc.sync, w3_s, 4, w3_scales)
         w2_raw = [load_w2(0)]
-        load_scale_rows(nc.sync, w_s, 0, w2_scales)
-        w1_raw = {(0, 0): load_w1(0, 0), (1, 0): load_w1(1, 0)}
-        nc.sync.dma_start(idx2[:], offs2)
-        wg = [load_wgs(0)]
+        w1_raw = {(0, 0): load_w1(0, 0)}
+        load_scale_rows(nc.sync, w2_s, 0, w2_scales)
         page = [load_page(0)]
-        nc.sync.dma_start(idx3[:], offs3)
+        nc.sync.dma_start(idx2[:], offs2)
+        w1_raw[(1, 0)] = load_w1(1, 0)
+        wg = [load_wgs(nc.gpsimd, 0)]
         load_gv()
+        nc.sync.dma_start(idx3[:], offs3)
         w3_raw.append(load_w3(1))
         w2_raw.append(load_w2(1))
         w1_raw[(0, 1)] = load_w1(0, 1)
         w1_raw[(1, 1)] = load_w1(1, 1)
         for t in range(1, PACK):
-            wg.append(load_wgs(t))
+            wg.append(load_wgs(nc.sync, t))
             page.append(load_page(t))
         for s in range(PACK, SLICES):
             page.append(load_page(s))
@@ -147,40 +150,28 @@ def tile_list_braille_cell_proofing_kernel(
             nc.vector.tensor_copy(words[:].bitcast(U32), tab_w[a][:].bitcast(U32).indirect(idx[:]))
             v_w.append(words)
 
-        w_sd = keep.tile([P, RP * PACK * KP * P], U8, name="w_sd", align_bytes=64)
-        nc.vector.tensor_copy(
-            w_sd[:].bitcast(I32).rearrange("p (b t a u) -> p b t a u", b=RP, t=PACK, a=KP),
-            w_s[:].bitcast(I32).rearrange("p (a b u t) -> p b t a u", a=KP, b=RP, t=PACK),
-        )
-
-        def deal_w23(b):
-            raw2, raw3 = w2_raw[b], w3_raw[b]
-            d2 = keep.tile([P, PACK * KP * P // 2], I32, name="w2_d%d" % b, align_bytes=64)
-            d3 = keep.tile([P, PACK * KP * P], I32, name="w3_d%d" % b, align_bytes=64)
+        def deal_scales(raw, name):
+            dealt = keep.tile([P, RP * PACK * KP * P], U8, name=name, align_bytes=64)
             nc.vector.tensor_copy(
-                d2[:].rearrange("p (t a u i) -> p t a u i", t=PACK, a=KP, i=RUN // 2),
-                raw2[:].rearrange("p a (u t i) -> p t a u i", t=PACK, i=RUN // 2),
+                dealt[:].bitcast(I32).rearrange("p (b t a u) -> p b t a u", b=RP, t=PACK, a=KP),
+                raw[:].bitcast(I32).rearrange("p (a b u t) -> p b t a u", a=KP, b=RP, t=PACK),
             )
+            return dealt
+
+        def deal_words(raw, run, name):
+            dealt = keep.tile([P, PACK * KP * RUNS * run], I32, name=name, align_bytes=64)
             nc.vector.tensor_copy(
-                d3[:].rearrange("p (t a u i) -> p t a u i", t=PACK, a=KP, i=RUN),
-                raw3[:].rearrange("p a (u t i) -> p t a u i", t=PACK, i=RUN),
+                dealt[:].rearrange("p (t a u i) -> p t a u i", t=PACK, a=KP, i=run),
+                raw[:].rearrange("p a (u t i) -> p t a u i", t=PACK, i=run),
             )
-            return d2, d3
+            return dealt
 
-        staging = {}
-        for kind, s in [("w1", 0), ("f3", 0)] + [(kind, s) for s in range(1, SLICES) for kind in ("f3", "w1")]:
-            shape, dtype = ([P, KP, P * PACK], BF16) if kind == "w1" else ([P, S], F32)
-            staging[(kind, s)] = ring.tile(shape, dtype, name="staging", tag="staging", bufs=2, align_bytes=64)
-
-        def cast_w1(s):
+        def cast_w1(s, a, copy, grouped):
             b, t = divmod(s, PACK)
-            grouped = staging[("w1", s)]
-            for a in range(KP):
-                nc.scalar.copy(
-                    grouped[:, a, :].rearrange("p (u i j) -> p u i j", i=RUN, j=PACK),
-                    w1_raw[(a, b)][:].rearrange("p j (u t i) -> p t u i j", t=PACK, i=RUN)[:, t],
-                )
-            return grouped
+            copy(
+                grouped.rearrange("p (u i j) -> p u i j", i=RUN, j=PACK),
+                w1_raw[(a, b)][:].rearrange("p j (u t i) -> p t u i j", t=PACK, i=RUN)[:, t],
+            )
 
         def quantize(grouped_ap, width, name, bufs):
             codes = ring.tile([P, width], U32, name=name + "_c", tag=name + "_c", bufs=bufs, align_bytes=64)
@@ -201,35 +192,44 @@ def tile_list_braille_cell_proofing_kernel(
 
         def lower_of_f2_f3(s):
             b, t = divmod(s, PACK)
-            d2, d3 = w23_d[b]
+            d2, d3 = w2_d[b], w3_d[b]
 
             def w2_of(a):
                 n = t * KP + a
                 m = s * KP + a
-                return (d2[:].bitcast(U8)[:, n * 2 * P : (n + 1) * 2 * P].bitcast(FP4X4), w_sd[:, m * P : (m + 1) * P])
+                return (d2[:].bitcast(U8)[:, n * 2 * P : (n + 1) * 2 * P].bitcast(FP4X4), w2_sd[:, m * P : (m + 1) * P])
 
             def w3_of(a):
                 n = t * KP + a
                 m = s * KP + a
-                return (d3[:, n * P : (n + 1) * P].bitcast(FP8X4), w_sd[4:P, m * P : (m + 1) * P])
+                return (d3[:, n * P : (n + 1) * P].bitcast(FP8X4), w3_sd[4:P, m * P : (m + 1) * P])
 
             f3 = stage1_product(2 * (s % 2), w3_of)
             f2 = stage1_product(2 * (s % 2) + 1, w2_of)
-            f3_sb = staging[("f3", s)]
+            f3_sb = ring.tile([P, S], F32, name="f3_sb", tag="f3_sb", bufs=FB)
             nc.scalar.copy(f3_sb[:], f3[:])
             low = ring.tile([P, S], F32, name="low", tag="low", bufs=LB)
             nc.vector.tensor_tensor(low[:], f2[:], f3_sb[:], ALU.min)
             return low
 
-        def quantize_w1(grouped):
-            return quantize(grouped[:].rearrange("p a c -> p (a c)"), KP * P, "w1", CB)
+        def quantize_w1(s):
+            grouped = ring.tile([P, KP, PASS], BF16, name="w1_bf", tag="w1_bf", bufs=WB, align_bytes=64)
+            for a in range(KP):
+                cast_w1(s, a, nc.scalar.copy, grouped[:, a, :])
+            codes, scales = quantize(grouped[:].rearrange("p a c -> p (a c)"), KP * P, "w1", CB)
+            return [(codes[:, a * P : (a + 1) * P].bitcast(FP8X4), scales[:, a * P : (a + 1) * P]) for a in range(KP)]
+
+        def quantize_w1_first():
+            passes = []
+            for a, copy in enumerate((nc.scalar.copy, nc.vector.tensor_copy)):
+                grouped = keep.tile([P, PASS], BF16, name="w1_first%d" % a, align_bytes=64)
+                cast_w1(0, a, copy, grouped[:])
+                codes, scales = quantize(grouped[:], P, "w1_first%d" % a, 1)
+                passes.append((codes[:].bitcast(FP8X4), scales[:]))
+            return passes
 
         def features(s, quantized, low):
-            codes, scales = quantized
-            f1 = stage1_product(
-                4 + s % F1B,
-                lambda a: (codes[:, a * P : (a + 1) * P].bitcast(FP8X4), scales[:, a * P : (a + 1) * P])
-            )
+            f1 = stage1_product(4 + s % F1B, lambda a: quantized[a])
             if s == SLICES - 1:
                 h = ring.tile([P, S], F32, name="h_last", tag="page_il3", bufs=1, align_bytes=64)
             else:
@@ -249,13 +249,16 @@ def tile_list_braille_cell_proofing_kernel(
             )
             return grouped[:].rearrange("p c t -> p (c t)")
 
-        w23_d = [deal_w23(0)]
+        w3_d = [deal_words(w3_raw[0], RUN, "w3_d0")]
+        w3_sd = deal_scales(w3_s, "w3_sd")
+        w2_d = [deal_words(w2_raw[0], RUN // 2, "w2_d0")]
+        w2_sd = deal_scales(w2_s, "w2_sd")
         lows = [lower_of_f2_f3(0)]
-        w1_q = [quantize_w1(cast_w1(0))]
+        w1_q = [quantize_w1_first()]
         hs = [features(0, w1_q[0], lows[0])]
         for s in range(1, 3):
             lows.append(lower_of_f2_f3(s))
-            w1_q.append(quantize_w1(cast_w1(s)))
+            w1_q.append(quantize_w1(s))
 
         page_q, x_q, page_bf, x_bf = [], [], [], []
         for s in range(SLICES):
@@ -267,12 +270,13 @@ def tile_list_braille_cell_proofing_kernel(
             if s + 1 < SLICES:
                 hs.append(features(s + 1, w1_q[s + 1], lows[s + 1]))
             if s == 0:
-                w23_d.append(deal_w23(1))
-                nc.vector.tensor_scalar(gv_pos[:], gv_cols, 0.0, 2.0, ALU.is_ge, ALU.mult)
-                nc.vector.tensor_scalar(gv_sign[:], gv_pos[:], 1.0, -1.0, ALU.mult, ALU.add)
+                w3_d.append(deal_words(w3_raw[1], RUN, "w3_d1"))
+                w2_d.append(deal_words(w2_raw[1], RUN // 2, "w2_d1"))
+                nc.gpsimd.tensor_scalar(gv_pos[:], gv_cols, 0.0, 2.0, ALU.is_ge, ALU.mult)
+                nc.gpsimd.tensor_scalar(gv_sign[:], gv_pos[:], 1.0, -1.0, ALU.mult, ALU.add)
             if s + 3 < SLICES:
                 lows.append(lower_of_f2_f3(s + 3))
-                w1_q.append(quantize_w1(cast_w1(s + 3)))
+                w1_q.append(quantize_w1(s + 3))
             nc.scalar.activation(page_bf[b][:, t, :], page[s][:], ACT.Copy, scale=gv_sign[:, b, t : t + 1])
             picked = ring.tile([P, NP], F32, name="picked", tag="picked", bufs=PB)
             nc.vector.tensor_copy(picked[:], page[s][:].indirect(idx3[:]))

@@ -17,16 +17,21 @@ ALU = mybir.AluOpType
 ACT = mybir.ActivationFunctionType
 
 P = 128
+QUAD = 32
 PACK = 4
 PASS = P * PACK
 KP = K // PASS
 RP = H // PASS
 RUN = 4
 RUNS = P // RUN
+SPAN = RUN * PACK
 SLICES = RP * PACK
-BANKS = 8
-QUART = T2 // 4
-HB, LB, CB, VABS, DB, F1B, PB, FB, WB = 1, 1, 1, (1, 3, 5, 7), 4, 1, 2, 1, 1
+AHEAD = 3
+PART = T2 // 4
+OUT_TILES = T2 // P
+F1_BANK = 4
+W3_ROW = 4
+OUT_BUFS = 4
 
 
 def tile_list_braille_cell_proofing_kernel(
@@ -46,9 +51,6 @@ def tile_list_braille_cell_proofing_kernel(
         idx2 = keep.tile([P, S // 16], U16, name="idx2")
         idx3 = keep.tile([P, NP // 16], U16, name="idx3")
 
-        warm = keep.tile([P, 8], F32, name="warm")
-        warm_out = keep.tile([P, 8], F32, name="warm_out")
-
         tab_s = keep.tile([P, KP * T], U8, name="tab_s", align_bytes=64)
         w2_s = keep.tile([P, KP * H], U8, name="w2_s", align_bytes=64)
         w3_s = keep.tile([P, KP * H], U8, name="w3_s", align_bytes=64)
@@ -56,19 +58,17 @@ def tile_list_braille_cell_proofing_kernel(
         nc.vector.memset(w3_s[:].bitcast(I32), 0)
         nc.vector.memset(w2_s[:].bitcast(I32), 0)
         v_s = [keep.tile([P, S], U8, name="v_s%d" % a, align_bytes=64) for a in range(KP)]
-        nc.vector.memset(warm[:], 0.0)
-        nc.scalar.activation(warm_out[:], warm[:], ACT.Exp)
 
         def load_tab_words(a):
             tile = keep.tile([P, T], I32, name="tab_w%d" % a, align_bytes=64)
             nc.sync.dma_start(tile[:], tab_words[a].rearrange("p t i -> p (t i)").bitcast(I32))
             return tile
 
-        def load_scale_rows(queue, tile, first_row, scales):
+        def load_scale_rows(tile, first_row, scales):
             rows = scales.bitcast(I32).rearrange("a q c -> q a c")
-            for quad in range(4):
-                lo = 32 * quad + first_row
-                queue.dma_start(
+            for quad in range(P // QUAD):
+                lo = QUAD * quad + first_row
+                nc.sync.dma_start(
                     tile[lo : lo + 4, :].bitcast(I32).rearrange("p (a c) -> p a c", a=KP),
                     rows[4 * quad : 4 * quad + 4],
                 )
@@ -85,8 +85,11 @@ def tile_list_braille_cell_proofing_kernel(
             nc.sync.dma_start(raw[:], src[:, :, b * PASS : (b + 1) * PASS])
             return raw
 
+        def float_block():
+            return ring.tile([P, PACK, PASS], F32, name="w1_raw", tag="w1_raw", bufs=KP * RP)
+
         def load_w1(a, b):
-            tile = ring.tile([P, PACK, PASS], F32, name="w1_raw", tag="w1_raw", bufs=4)
+            tile = float_block()
             rows = w1[a * PASS : (a + 1) * PASS, b * PASS : (b + 1) * PASS]
             nc.sync.dma_start(tile[:], rows.rearrange("(p j) c -> p j c", j=PACK))
             return tile
@@ -94,8 +97,8 @@ def tile_list_braille_cell_proofing_kernel(
         def load_wgs(queue, t):
             tile = keep.tile([P, S], F32, name="wg%d" % t)
             rows = wgs.rearrange("(u t i) j -> t u i j", t=PACK, i=RUN)[t]
-            for quad in range(4):
-                queue.dma_start(tile[32 * quad : 32 * quad + 32, :], rows)
+            for quad in range(P // QUAD):
+                queue.dma_start(tile[QUAD * quad : QUAD * quad + QUAD, :], rows)
             return tile
 
         def load_page(s):
@@ -104,28 +107,28 @@ def tile_list_braille_cell_proofing_kernel(
             nc.sync.dma_start(tile[:], page0.rearrange("(b u t i) m -> b t u i m", b=RP, t=PACK, i=RUN)[b, t])
             return tile
 
-        gv_run = keep.tile([P, RP, 16], F32, name="gv_run")
+        gv_run = keep.tile([P, RP, SPAN], F32, name="gv_run")
+        gv_len = SPAN - RUN + 1
 
         def load_gv():
-            rows = gv.rearrange("(b u c) -> u b c", b=RP, c=16)
+            rows = gv.rearrange("(b u c) -> u b c", b=RP, c=SPAN)
             for i in range(RUN):
-                nc.gpsimd.dma_start(gv_run[i:P:RUN, :, 0:13], rows[:, :, i : i + 13])
+                nc.gpsimd.dma_start(gv_run[i:P:RUN, :, 0:gv_len], rows[:, :, i : i + gv_len])
 
         def load_ref(half):
-            tile = ring.tile([P, PACK, PASS], F32, name="w1_raw", tag="w1_raw", bufs=4)
-            rows = ref[half * 512 : (half + 1) * 512, :].rearrange("(m p) j -> p m j", p=P)
+            tile = float_block()
+            rows = ref[half * PASS : (half + 1) * PASS, :].rearrange("(n p) j -> p n j", p=P)
             nc.sync.dma_start(tile[:], rows)
             return tile
 
         nc.sync.dma_start(idx[:], offs)
-        load_scale_rows(nc.sync, tab_s, 0, tab_scales)
-        tab_w = [load_tab_words(0)]
-        tab_w.append(load_tab_words(1))
+        load_scale_rows(tab_s, 0, tab_scales)
+        tab_w = [load_tab_words(a) for a in range(KP)]
         w3_raw = [load_w3(0)]
-        load_scale_rows(nc.sync, w3_s, 4, w3_scales)
+        load_scale_rows(w3_s, W3_ROW, w3_scales)
         w2_raw = [load_w2(0)]
         w1_raw = {(0, 0): load_w1(0, 0)}
-        load_scale_rows(nc.sync, w2_s, 0, w2_scales)
+        load_scale_rows(w2_s, 0, w2_scales)
         page = [load_page(0)]
         nc.sync.dma_start(idx2[:], offs2)
         w1_raw[(1, 0)] = load_w1(1, 0)
@@ -134,8 +137,8 @@ def tile_list_braille_cell_proofing_kernel(
         nc.sync.dma_start(idx3[:], offs3)
         w3_raw.append(load_w3(1))
         w2_raw.append(load_w2(1))
-        w1_raw[(0, 1)] = load_w1(0, 1)
-        w1_raw[(1, 1)] = load_w1(1, 1)
+        for a in range(KP):
+            w1_raw[(a, 1)] = load_w1(a, 1)
         for t in range(1, PACK):
             wg.append(load_wgs(nc.sync, t))
             page.append(load_page(t))
@@ -158,31 +161,30 @@ def tile_list_braille_cell_proofing_kernel(
             )
             return dealt
 
-        def deal_words(raw, run, name):
-            dealt = keep.tile([P, PACK * KP * RUNS * run], I32, name=name, align_bytes=64)
+        def deal_words(raw, run_words, name):
+            dealt = keep.tile([P, PACK * KP * RUNS * run_words], I32, name=name, align_bytes=64)
             nc.vector.tensor_copy(
-                dealt[:].rearrange("p (t a u i) -> p t a u i", t=PACK, a=KP, i=run),
-                raw[:].rearrange("p a (u t i) -> p t a u i", t=PACK, i=run),
+                dealt[:].rearrange("p (t a u i) -> p t a u i", t=PACK, a=KP, i=run_words),
+                raw[:].rearrange("p a (u t i) -> p t a u i", t=PACK, i=run_words),
             )
             return dealt
 
-        def cast_w1(s, a, copy, grouped):
+        def round_w1(s, a, copy, grouped):
             b, t = divmod(s, PACK)
             copy(
                 grouped.rearrange("p (u i j) -> p u i j", i=RUN, j=PACK),
                 w1_raw[(a, b)][:].rearrange("p j (u t i) -> p t u i j", t=PACK, i=RUN)[:, t],
             )
 
-        def quantize(grouped_ap, width, name, bufs):
+        def quantize(grouped, width, name, bufs):
             codes = ring.tile([P, width], U32, name=name + "_c", tag=name + "_c", bufs=bufs, align_bytes=64)
             scales = ring.tile([P, width], U8, name=name + "_s", tag=name + "_s", bufs=bufs, align_bytes=64)
-            nc.vector.quantize_mx(out=codes[:].bitcast(FP8X4), scales=scales[:], in_=grouped_ap)
+            nc.vector.quantize_mx(out=codes[:].bitcast(FP8X4), scales=scales[:], in_=grouped)
             return codes, scales
 
-        def stage1_product(n, lhs_of_pass):
-            bank = bank_tile(n)
-            for a in range(KP):
-                codes, scales = lhs_of_pass(a)
+        def product_with_table(bank_number, weight_passes):
+            bank = bank_tile(bank_number)
+            for a, (codes, scales) in enumerate(weight_passes):
                 nc.tensor.matmul_mx(
                     out=bank[:], lhsT=codes, lhsT_scale=scales,
                     rhs=v_w[a][:].bitcast(FP8X4), rhs_scale=v_s[a][:],
@@ -192,62 +194,65 @@ def tile_list_braille_cell_proofing_kernel(
 
         def lower_of_f2_f3(s):
             b, t = divmod(s, PACK)
-            d2, d3 = w2_d[b], w3_d[b]
-
-            def w2_of(a):
+            w2_passes, w3_passes = [], []
+            for a in range(KP):
                 n = t * KP + a
-                m = s * KP + a
-                return (d2[:].bitcast(U8)[:, n * 2 * P : (n + 1) * 2 * P].bitcast(FP4X4), w2_sd[:, m * P : (m + 1) * P])
-
-            def w3_of(a):
-                n = t * KP + a
-                m = s * KP + a
-                return (d3[:, n * P : (n + 1) * P].bitcast(FP8X4), w3_sd[4:P, m * P : (m + 1) * P])
-
-            f3 = stage1_product(2 * (s % 2), w3_of)
-            f2 = stage1_product(2 * (s % 2) + 1, w2_of)
-            f3_sb = ring.tile([P, S], F32, name="f3_sb", tag="f3_sb", bufs=FB)
+                scale_cols = slice((s * KP + a) * P, (s * KP + a + 1) * P)
+                w2_codes = w2_d[b][:].bitcast(U8)[:, n * 2 * P : (n + 1) * 2 * P].bitcast(FP4X4)
+                w2_passes.append((w2_codes, w2_sd[:, scale_cols]))
+                w3_passes.append((w3_d[b][:, n * P : (n + 1) * P].bitcast(FP8X4), w3_sd[W3_ROW:P, scale_cols]))
+            f3 = product_with_table(2 * (s % 2), w3_passes)
+            f2 = product_with_table(2 * (s % 2) + 1, w2_passes)
+            f3_sb = ring.tile([P, S], F32, name="f3_sb", tag="f3_sb", bufs=1)
             nc.scalar.copy(f3_sb[:], f3[:])
-            low = ring.tile([P, S], F32, name="low", tag="low", bufs=LB)
+            low = ring.tile([P, S], F32, name="low", tag="low", bufs=1)
             nc.vector.tensor_tensor(low[:], f2[:], f3_sb[:], ALU.min)
             return low
 
         def quantize_w1(s):
-            grouped = ring.tile([P, KP, PASS], BF16, name="w1_bf", tag="w1_bf", bufs=WB, align_bytes=64)
+            grouped = ring.tile([P, KP, PASS], BF16, name="w1_bf", tag="w1_bf", bufs=1, align_bytes=64)
             for a in range(KP):
-                cast_w1(s, a, nc.scalar.copy, grouped[:, a, :])
-            codes, scales = quantize(grouped[:].rearrange("p a c -> p (a c)"), KP * P, "w1", CB)
+                round_w1(s, a, nc.scalar.copy, grouped[:, a, :])
+            codes, scales = quantize(grouped[:].rearrange("p a c -> p (a c)"), KP * P, "w1", 1)
             return [(codes[:, a * P : (a + 1) * P].bitcast(FP8X4), scales[:, a * P : (a + 1) * P]) for a in range(KP)]
 
         def quantize_w1_first():
             passes = []
             for a, copy in enumerate((nc.scalar.copy, nc.vector.tensor_copy)):
                 grouped = keep.tile([P, PASS], BF16, name="w1_first%d" % a, align_bytes=64)
-                cast_w1(0, a, copy, grouped[:])
+                round_w1(0, a, copy, grouped[:])
                 codes, scales = quantize(grouped[:], P, "w1_first%d" % a, 1)
                 passes.append((codes[:].bitcast(FP8X4), scales[:]))
             return passes
 
-        def features(s, quantized, low):
-            f1 = stage1_product(4 + s % F1B, lambda a: quantized[a])
+        def features(s, w1_passes, low):
+            f1 = product_with_table(F1_BANK, w1_passes)
             if s == SLICES - 1:
                 h = ring.tile([P, S], F32, name="h_last", tag="page_il3", bufs=1, align_bytes=64)
             else:
-                h = ring.tile([P, S], F32, name="h", tag="h", bufs=HB)
+                h = ring.tile([P, S], F32, name="h", tag="h", bufs=1)
             nc.vector.tensor_tensor(h[:], f1[:], low[:], ALU.max)
             return h
 
-        gv_cols = gv_run[:, :, 0:13:PACK]
         gv_pos = keep.tile([P, RP, PACK], F32, name="gv_pos")
         gv_sign = keep.tile([P, RP, PACK], F32, name="gv_sign")
 
-        def interleave(copy, planes, columns, name):
+        def interleave(copy, by_slice, columns, name):
             grouped = ring.tile([P, columns.stop - columns.start, PACK], BF16, name=name, tag=name, bufs=1, align_bytes=64)
             copy(
                 grouped[:].rearrange("p (c i) t -> p c t i", i=4),
-                planes[:, :, columns].rearrange("p t (c i) -> p c t i", i=4),
+                by_slice[:, :, columns].rearrange("p t (c i) -> p c t i", i=4),
             )
             return grouped[:].rearrange("p c t -> p (c t)")
+
+        def quantize_pass(b):
+            first = nc.scalar.copy if b == 0 else nc.vector.tensor_copy
+            parts = [interleave(first, page_bf[b], slice(0, PART), "page_il0")]
+            x_il = interleave(first, x_bf[b], slice(0, NP), "x_il")
+            for n in range(1, T2 // PART):
+                parts.append(interleave(nc.scalar.copy, page_bf[b], slice(n * PART, (n + 1) * PART), "page_il%d" % n))
+            x_q.append(quantize(x_il, NP, "x", RP))
+            page_q.append([quantize(part, PART, "page", RP * T2 // PART) for part in parts])
 
         w3_d = [deal_words(w3_raw[0], RUN, "w3_d0")]
         w3_sd = deal_scales(w3_s, "w3_sd")
@@ -256,7 +261,7 @@ def tile_list_braille_cell_proofing_kernel(
         lows = [lower_of_f2_f3(0)]
         w1_q = [quantize_w1_first()]
         hs = [features(0, w1_q[0], lows[0])]
-        for s in range(1, 3):
+        for s in range(1, AHEAD):
             lows.append(lower_of_f2_f3(s))
             w1_q.append(quantize_w1(s))
 
@@ -272,44 +277,39 @@ def tile_list_braille_cell_proofing_kernel(
             if s == 0:
                 w3_d.append(deal_words(w3_raw[1], RUN, "w3_d1"))
                 w2_d.append(deal_words(w2_raw[1], RUN // 2, "w2_d1"))
-                nc.gpsimd.tensor_scalar(gv_pos[:], gv_cols, 0.0, 2.0, ALU.is_ge, ALU.mult)
+                nc.gpsimd.tensor_scalar(gv_pos[:], gv_run[:, :, 0:gv_len:RUN], 0.0, 2.0, ALU.is_ge, ALU.mult)
                 nc.gpsimd.tensor_scalar(gv_sign[:], gv_pos[:], 1.0, -1.0, ALU.mult, ALU.add)
-            if s + 3 < SLICES:
-                lows.append(lower_of_f2_f3(s + 3))
-                w1_q.append(quantize_w1(s + 3))
+            if s + AHEAD < SLICES:
+                lows.append(lower_of_f2_f3(s + AHEAD))
+                w1_q.append(quantize_w1(s + AHEAD))
             nc.scalar.activation(page_bf[b][:, t, :], page[s][:], ACT.Copy, scale=gv_sign[:, b, t : t + 1])
-            picked = ring.tile([P, NP], F32, name="picked", tag="picked", bufs=PB)
+            picked = ring.tile([P, NP], F32, name="picked", tag="picked", bufs=2)
             nc.vector.tensor_copy(picked[:], page[s][:].indirect(idx3[:]))
-            nc.scalar.activation(x_bf[b][:, t, :], picked[:], ACT.Abs, scale=gv_run[:, b, PACK * t : PACK * t + 1])
-            if s in (PACK, SLICES - 1):
-                b = len(x_q)
-                first = nc.scalar.copy if b == 0 else nc.vector.tensor_copy
-                parts = [interleave(first, page_bf[b], slice(0, QUART), "page_il0")]
-                x_il = interleave(first, x_bf[b], slice(0, NP), "x_il")
-                for n in range(1, 4):
-                    parts.append(interleave(nc.scalar.copy, page_bf[b], slice(n * QUART, (n + 1) * QUART), "page_il%d" % n))
-                x_q.append(quantize(x_il, NP, "x", 2))
-                page_q.append([quantize(part, QUART, "page", 8) for part in parts])
+            nc.scalar.activation(x_bf[b][:, t, :], picked[:], ACT.Abs, scale=gv_run[:, b, RUN * t : RUN * t + 1])
+            if s == PACK:
+                quantize_pass(0)
+        quantize_pass(1)
 
-        ref_sb = [load_ref(0), load_ref(1)]
-        scores = [bank_tile(m) for m in range(T2 // P)]
+        ref_sb = [load_ref(half) for half in range(T2 // PASS)]
+        scores = [bank_tile(m) for m in range(OUT_TILES)]
         for b in range(RP):
-            for m in range(T2 // P):
-                codes, scales = page_q[b][m // 2]
-                cols = slice((m % 2) * P, (m % 2 + 1) * P)
+            for m in range(OUT_TILES):
+                part, place = divmod(m, PART // P)
+                codes, scales = page_q[b][part]
+                cols = slice(place * P, (place + 1) * P)
                 nc.tensor.matmul_mx(
                     out=scores[m][:], lhsT=codes[:, cols].bitcast(FP8X4), lhsT_scale=scales[:, cols],
                     rhs=x_q[b][0][:].bitcast(FP8X4), rhs_scale=x_q[b][1][:],
                     start=(b == 0), stop=(b == RP - 1),
                 )
-        for m in range(T2 // P):
-            diff = ring.tile([P, NP], F32, name="diff", tag="diff", bufs=DB)
-            nc.vector.tensor_tensor(diff[:], scores[m][:], ref_sb[m // 4][:, m % 4, :], ALU.subtract)
-            size = ring.tile([P, NP], F32, name="size", tag="size", bufs=DB)
-            if m not in VABS:
+        for m in range(OUT_TILES):
+            diff = ring.tile([P, NP], F32, name="diff", tag="diff", bufs=OUT_BUFS)
+            nc.vector.tensor_tensor(diff[:], scores[m][:], ref_sb[m // PACK][:, m % PACK, :], ALU.subtract)
+            size = ring.tile([P, NP], F32, name="size", tag="size", bufs=OUT_BUFS)
+            if m % 2 == 0:
                 nc.scalar.activation(size[:], diff[:], ACT.Abs)
             else:
                 nc.vector.scalar_tensor_tensor(size[:], diff[:], -1.0, diff[:], ALU.mult, ALU.max)
-            result = ring.tile([P, NP], F32, name="result", tag="result", bufs=DB)
+            result = ring.tile([P, NP], F32, name="result", tag="result", bufs=OUT_BUFS)
             nc.scalar.activation(result[:], size[:], ACT.Exp, scale=-1.0)
             nc.sync.dma_start(out[m * P : (m + 1) * P, :], result[:])

from contextlib import ExitStack

import concourse.mybir as mybir

K, H, T, S, T2, NP = 1024, 1024, 2048, 512, 1024, 512
FLOPS = 2 * (3 * K * H * S + H * T2 * NP)

F32 = mybir.dt.float32
BF16 = mybir.dt.bfloat16
I32 = mybir.dt.int32
U32 = mybir.dt.uint32
U16 = mybir.dt.uint16
U8 = mybir.dt.uint8
FP8X4 = mybir.dt.float8_e4m3fn_x4
FP4X4 = mybir.dt.float4_e2m1fn_x4
ALU = mybir.AluOpType
ACT = mybir.ActivationFunctionType

P = 128
QUAD = 32
PACK = 4
PASS = P * PACK
KP = K // PASS
RP = H // PASS
RUN = 4
RUNS = P // RUN
SPAN = RUN * PACK
SLICES = RP * PACK
AHEAD = 3
PART = T2 // 4
OUT_TILES = T2 // P
F1_BANK = 4
W3_ROW = 4
OUT_BUFS = 4


def tile_list_braille_cell_proofing_kernel(
    tc, tab_words, tab_scales, offs, w1, w2_words, w2_scales, w3_words, w3_scales,
    wgs, page0, offs2, offs3, gv, ref, out,
):
    nc = tc.nc
    with ExitStack() as ctx:
        keep = ctx.enter_context(tc.tile_pool(name="keep", bufs=1))
        ring = ctx.enter_context(tc.tile_pool(name="ring", bufs=2))
        psum = ctx.enter_context(tc.psum_pool(name="psum", bufs=1))

        def bank_tile(n):
            return psum.tile([P, 512], F32, name="bank%d" % n)

        idx = keep.tile([P, S // 16], U16, name="idx")
        idx2 = keep.tile([P, S // 16], U16, name="idx2")
        idx3 = keep.tile([P, NP // 16], U16, name="idx3")

        tab_s = keep.tile([P, KP * T], U8, name="tab_s", align_bytes=64)
        w2_s = keep.tile([P, KP * H], U8, name="w2_s", align_bytes=64)
        w3_s = keep.tile([P, KP * H], U8, name="w3_s", align_bytes=64)
        nc.vector.memset(tab_s[:].bitcast(I32), 0)
        nc.vector.memset(w3_s[:].bitcast(I32), 0)
        nc.vector.memset(w2_s[:].bitcast(I32), 0)
        v_s = [keep.tile([P, S], U8, name="v_s%d" % a, align_bytes=64) for a in range(KP)]

        def load_tab_words(a):
            tile = keep.tile([P, T], I32, name="tab_w%d" % a, align_bytes=64)
            nc.sync.dma_start(tile[:], tab_words[a].rearrange("p t i -> p (t i)").bitcast(I32))
            return tile

        def load_scale_rows(tile, first_row, scales):
            rows = scales.bitcast(I32).rearrange("a q c -> q a c")
            for quad in range(P // QUAD):
                lo = QUAD * quad + first_row
                nc.sync.dma_start(
                    tile[lo : lo + 4, :].bitcast(I32).rearrange("p (a c) -> p a c", a=KP),
                    rows[4 * quad : 4 * quad + 4],
                )

        def load_w2(b):
            raw = keep.tile([P, KP, PASS // 2], I32, name="w2_raw%d" % b)
            src = w2_words.bitcast(I32).rearrange("a p c -> p a c")
            nc.sync.dma_start(raw[:], src[:, :, b * PASS // 2 : (b + 1) * PASS // 2])
            return raw

        def load_w3(b):
            raw = keep.tile([P, KP, PASS], I32, name="w3_raw%d" % b)
            src = w3_words.rearrange("a p c i -> a p (c i)").bitcast(I32).rearrange("a p c -> p a c")
            nc.sync.dma_start(raw[:], src[:, :, b * PASS : (b + 1) * PASS])
            return raw

        def float_block():
            return ring.tile([P, PACK, PASS], F32, name="w1_raw", tag="w1_raw", bufs=KP * RP)

        def load_w1(a, b):
            tile = float_block()
            rows = w1[a * PASS : (a + 1) * PASS, b * PASS : (b + 1) * PASS]
            nc.sync.dma_start(tile[:], rows.rearrange("(p j) c -> p j c", j=PACK))
            return tile

        def load_wgs(queue, t):
            tile = keep.tile([P, S], F32, name="wg%d" % t)
            rows = wgs.rearrange("(u t i) j -> t u i j", t=PACK, i=RUN)[t]
            for quad in range(P // QUAD):
                queue.dma_start(tile[QUAD * quad : QUAD * quad + QUAD, :], rows)
            return tile

        def load_page(s):
            b, t = divmod(s, PACK)
            tile = keep.tile([P, T2], F32, name="page%d" % s)
            nc.sync.dma_start(tile[:], page0.rearrange("(b u t i) m -> b t u i m", b=RP, t=PACK, i=RUN)[b, t])
            return tile

        gv_run = keep.tile([P, RP, SPAN], F32, name="gv_run")
        gv_len = SPAN - RUN + 1

        def load_gv():
            rows = gv.rearrange("(b u c) -> u b c", b=RP, c=SPAN)
            for i in range(RUN):
                nc.gpsimd.dma_start(gv_run[i:P:RUN, :, 0:gv_len], rows[:, :, i : i + gv_len])

        def load_ref(half):
            tile = float_block()
            rows = ref[half * PASS : (half + 1) * PASS, :].rearrange("(n p) j -> p n j", p=P)
            nc.sync.dma_start(tile[:], rows)
            return tile

        nc.sync.dma_start(idx[:], offs)
        load_scale_rows(tab_s, 0, tab_scales)
        tab_w = [load_tab_words(a) for a in range(KP)]
        w3_raw = [load_w3(0)]
        load_scale_rows(w3_s, W3_ROW, w3_scales)
        w2_raw = [load_w2(0)]
        w1_raw = {(0, 0): load_w1(0, 0)}
        load_scale_rows(w2_s, 0, w2_scales)
        page = [load_page(0)]
        nc.sync.dma_start(idx2[:], offs2)
        w1_raw[(1, 0)] = load_w1(1, 0)
        wg = [load_wgs(nc.gpsimd, 0)]
        load_gv()
        nc.sync.dma_start(idx3[:], offs3)
        w3_raw.append(load_w3(1))
        w2_raw.append(load_w2(1))
        for a in range(KP):
            w1_raw[(a, 1)] = load_w1(a, 1)
        for t in range(1, PACK):
            wg.append(load_wgs(nc.sync, t))
            page.append(load_page(t))
        for s in range(PACK, SLICES):
            page.append(load_page(s))

        for a in range(KP):
            nc.vector.tensor_copy(v_s[a][:], tab_s[:, a * T : (a + 1) * T].indirect(idx[:]))
        v_w = []
        for a in range(KP):
            words = keep.tile([P, S], I32, name="v_w%d" % a, align_bytes=64)
            nc.vector.tensor_copy(words[:].bitcast(U32), tab_w[a][:].bitcast(U32).indirect(idx[:]))
            v_w.append(words)

        def deal_scales(raw, name):
            dealt = keep.tile([P, RP * PACK * KP * P], U8, name=name, align_bytes=64)
            nc.vector.tensor_copy(
                dealt[:].bitcast(I32).rearrange("p (b t a u) -> p b t a u", b=RP, t=PACK, a=KP),
                raw[:].bitcast(I32).rearrange("p (a b u t) -> p b t a u", a=KP, b=RP, t=PACK),
            )
            return dealt

        def deal_words(raw, run_words, name):
            dealt = keep.tile([P, PACK * KP * RUNS * run_words], I32, name=name, align_bytes=64)
            nc.vector.tensor_copy(
                dealt[:].rearrange("p (t a u i) -> p t a u i", t=PACK, a=KP, i=run_words),
                raw[:].rearrange("p a (u t i) -> p t a u i", t=PACK, i=run_words),
            )
            return dealt

        def round_w1(s, a, copy, grouped):
            b, t = divmod(s, PACK)
            copy(
                grouped.rearrange("p (u i j) -> p u i j", i=RUN, j=PACK),
                w1_raw[(a, b)][:].rearrange("p j (u t i) -> p t u i j", t=PACK, i=RUN)[:, t],
            )

        def quantize(grouped, width, name, bufs):
            codes = ring.tile([P, width], U32, name=name + "_c", tag=name + "_c", bufs=bufs, align_bytes=64)
            scales = ring.tile([P, width], U8, name=name + "_s", tag=name + "_s", bufs=bufs, align_bytes=64)
            nc.vector.quantize_mx(out=codes[:].bitcast(FP8X4), scales=scales[:], in_=grouped)
            return codes, scales

        def product_with_table(bank_number, weight_passes):
            bank = bank_tile(bank_number)
            for a, (codes, scales) in enumerate(weight_passes):
                nc.tensor.matmul_mx(
                    out=bank[:], lhsT=codes, lhsT_scale=scales,
                    rhs=v_w[a][:].bitcast(FP8X4), rhs_scale=v_s[a][:],
                    start=(a == 0), stop=(a == KP - 1),
                )
            return bank

        def lower_of_f2_f3(s):
            b, t = divmod(s, PACK)
            w2_passes, w3_passes = [], []
            for a in range(KP):
                n = t * KP + a
                scale_cols = slice((s * KP + a) * P, (s * KP + a + 1) * P)
                w2_codes = w2_d[b][:].bitcast(U8)[:, n * 2 * P : (n + 1) * 2 * P].bitcast(FP4X4)
                w2_passes.append((w2_codes, w2_sd[:, scale_cols]))
                w3_passes.append((w3_d[b][:, n * P : (n + 1) * P].bitcast(FP8X4), w3_sd[W3_ROW:P, scale_cols]))
            f3 = product_with_table(2 * (s % 2), w3_passes)
            f2 = product_with_table(2 * (s % 2) + 1, w2_passes)
            f3_sb = ring.tile([P, S], F32, name="f3_sb", tag="f3_sb", bufs=1)
            nc.scalar.copy(f3_sb[:], f3[:])
            low = ring.tile([P, S], F32, name="low", tag="low", bufs=1)
            nc.vector.tensor_tensor(low[:], f2[:], f3_sb[:], ALU.min)
            return low

        def quantize_w1(s):
            grouped = ring.tile([P, KP, PASS], BF16, name="w1_bf", tag="w1_bf", bufs=1, align_bytes=64)
            for a in range(KP):
                round_w1(s, a, nc.scalar.copy, grouped[:, a, :])
            codes, scales = quantize(grouped[:].rearrange("p a c -> p (a c)"), KP * P, "w1", 1)
            return [(codes[:, a * P : (a + 1) * P].bitcast(FP8X4), scales[:, a * P : (a + 1) * P]) for a in range(KP)]

        def quantize_w1_first():
            passes = []
            for a, copy in enumerate((nc.scalar.copy, nc.vector.tensor_copy)):
                grouped = keep.tile([P, PASS], BF16, name="w1_first%d" % a, align_bytes=64)
                round_w1(0, a, copy, grouped[:])
                codes, scales = quantize(grouped[:], P, "w1_first%d" % a, 1)
                passes.append((codes[:].bitcast(FP8X4), scales[:]))
            return passes

        def features(s, w1_passes, low):
            f1 = product_with_table(F1_BANK, w1_passes)
            if s == SLICES - 1:
                h = ring.tile([P, S], F32, name="h_last", tag="page_il3", bufs=1, align_bytes=64)
            else:
                h = ring.tile([P, S], F32, name="h", tag="h", bufs=1)
            nc.vector.tensor_tensor(h[:], f1[:], low[:], ALU.max)
            return h

        gv_pos = keep.tile([P, RP, PACK], F32, name="gv_pos")
        gv_sign = keep.tile([P, RP, PACK], F32, name="gv_sign")

        def interleave(copy, by_slice, columns, name):
            grouped = ring.tile([P, columns.stop - columns.start, PACK], BF16, name=name, tag=name, bufs=1, align_bytes=64)
            copy(
                grouped[:].rearrange("p (c i) t -> p c t i", i=4),
                by_slice[:, :, columns].rearrange("p t (c i) -> p c t i", i=4),
            )
            return grouped[:].rearrange("p c t -> p (c t)")

        def quantize_pass(b):
            first = nc.scalar.copy if b == 0 else nc.vector.tensor_copy
            parts = [interleave(first, page_bf[b], slice(0, PART), "page_il0")]
            x_il = interleave(first, x_bf[b], slice(0, NP), "x_il")
            for n in range(1, T2 // PART):
                parts.append(interleave(nc.scalar.copy, page_bf[b], slice(n * PART, (n + 1) * PART), "page_il%d" % n))
            x_q.append(quantize(x_il, NP, "x", RP))
            page_q.append([quantize(part, PART, "page", RP * T2 // PART) for part in parts])

        w3_d = [deal_words(w3_raw[0], RUN, "w3_d0")]
        w3_sd = deal_scales(w3_s, "w3_sd")
        w2_d = [deal_words(w2_raw[0], RUN // 2, "w2_d0")]
        w2_sd = deal_scales(w2_s, "w2_sd")
        lows = [lower_of_f2_f3(0)]
        w1_q = [quantize_w1_first()]
        hs = [features(0, w1_q[0], lows[0])]
        for s in range(1, AHEAD):
            lows.append(lower_of_f2_f3(s))
            w1_q.append(quantize_w1(s))

        page_q, x_q, page_bf, x_bf = [], [], [], []
        for s in range(SLICES):
            b, t = divmod(s, PACK)
            if t == 0:
                page_bf.append(keep.tile([P, PACK, T2], BF16, name="page_bf%d" % b))
                x_bf.append(keep.tile([P, PACK, NP], BF16, name="x_bf%d" % b))
            nc.vector.tensor_tensor(page[s][:].indirect(idx2[:]), hs[s][:], wg[t][:], ALU.mult)
            if s + 1 < SLICES:
                hs.append(features(s + 1, w1_q[s + 1], lows[s + 1]))
            if s == 0:
                w3_d.append(deal_words(w3_raw[1], RUN, "w3_d1"))
                w2_d.append(deal_words(w2_raw[1], RUN // 2, "w2_d1"))
                nc.gpsimd.tensor_scalar(gv_pos[:], gv_run[:, :, 0:gv_len:RUN], 0.0, 2.0, ALU.is_ge, ALU.mult)
                nc.gpsimd.tensor_scalar(gv_sign[:], gv_pos[:], 1.0, -1.0, ALU.mult, ALU.add)
            if s + AHEAD < SLICES:
                lows.append(lower_of_f2_f3(s + AHEAD))
                w1_q.append(quantize_w1(s + AHEAD))
            nc.scalar.activation(page_bf[b][:, t, :], page[s][:], ACT.Copy, scale=gv_sign[:, b, t : t + 1])
            picked = ring.tile([P, NP], F32, name="picked", tag="picked", bufs=2)
            nc.vector.tensor_copy(picked[:], page[s][:].indirect(idx3[:]))
            nc.scalar.activation(x_bf[b][:, t, :], picked[:], ACT.Abs, scale=gv_run[:, b, RUN * t : RUN * t + 1])
            if s == PACK:
                quantize_pass(0)
        quantize_pass(1)

        ref_sb = [load_ref(half) for half in range(T2 // PASS)]
        scores = [bank_tile(m) for m in range(OUT_TILES)]
        for b in range(RP):
            for m in range(OUT_TILES):
                part, place = divmod(m, PART // P)
                codes, scales = page_q[b][part]
                cols = slice(place * P, (place + 1) * P)
                nc.tensor.matmul_mx(
                    out=scores[m][:], lhsT=codes[:, cols].bitcast(FP8X4), lhsT_scale=scales[:, cols],
                    rhs=x_q[b][0][:].bitcast(FP8X4), rhs_scale=x_q[b][1][:],
                    start=(b == 0), stop=(b == RP - 1),
                )
        for m in range(OUT_TILES):
            diff = ring.tile([P, NP], F32, name="diff", tag="diff", bufs=OUT_BUFS)
            nc.vector.tensor_tensor(diff[:], scores[m][:], ref_sb[m // PACK][:, m % PACK, :], ALU.subtract)
            size = ring.tile([P, NP], F32, name="size", tag="size", bufs=OUT_BUFS)
            if m % 2 == 0:
                nc.scalar.activation(size[:], diff[:], ACT.Abs)
            else:
                nc.vector.scalar_tensor_tensor(size[:], diff[:], -1.0, diff[:], ALU.mult, ALU.max)
            result = ring.tile([P, NP], F32, name="result", tag="result", bufs=OUT_BUFS)
            nc.scalar.activation(result[:], size[:], ACT.Exp, scale=-1.0)
            nc.sync.dma_start(out[m * P : (m + 1) * P, :], result[:])
